import numpy as np
import ml_dtypes


def mxq(x, axis, fmt="e4m3"):
    dtype, down = {"e4m3": (ml_dtypes.float8_e4m3fn, 7), "e5m2": (ml_dtypes.float8_e5m2, 14)}[fmt]
    v = np.moveaxis(np.asarray(x, np.float32).astype(ml_dtypes.bfloat16).astype(np.float64), axis, -1)
    blocks = v.reshape(v.shape[:-1] + (-1, 32))
    amax = np.abs(blocks).max(-1, keepdims=True)
    byte = np.maximum(np.where(amax > 0, np.frexp(amax)[1] - 1 + 127, 0) - down, 1)
    scale = np.exp2(byte - 127.0)
    codes = (blocks / scale).astype(np.float32).astype(dtype).astype(np.float64)
    return np.moveaxis((codes * scale).reshape(v.shape), -1, axis)


WIDE = False


def mx_kscale(k):
    if not WIDE:
        return np.ones(k)
    levels = np.array([10, -10, 5, -5, 0])
    if k % 512:
        return np.exp2(np.random.permutation(np.resize(levels, k // 32))).repeat(32)
    a = np.empty((k // 512, 16))
    for p in range(k // 512):
        a[p, :8] = np.random.permutation(np.resize(levels, 8))
        for g in range(8):
            far = levels[np.abs(levels - a[p, g]) >= 10]
            a[p, g + 8] = far[np.random.randint(len(far))]
    return np.exp2(a.ravel()).repeat(32)


BF16 = ml_dtypes.bfloat16


def bf(x):
    return np.asarray(x, np.float32).astype(BF16)


def f64(x):
    return np.asarray(x).astype(np.float64)


E2M1 = np.array([0.0, 0.5, 1.0, 1.5, 2.0, 3.0, 4.0, 6.0, -0.0, -0.5, -1.0, -1.5, -2.0, -3.0, -4.0, -6.0])


def pack_weight(w, fmt):
    k, n = w.shape
    w = f64(bf(w)).reshape(k // 32, 32, n)
    amax = np.abs(w).max(1)
    if fmt == "e4m3":
        byte = np.frexp(amax)[1] - 1 + 127 - 7
    else:
        mant, ex = np.frexp(amax / 6.0)
        byte = np.where(mant > 0.5, ex, ex - 1) + 127
    byte = np.clip(np.where(amax > 0, byte, 1), 1, 254)
    scaled = (w * np.exp2(127.0 - byte)[:, None, :]).reshape(k, n).astype(np.float32)
    by_word = np.ascontiguousarray(scaled.reshape(k // 512, 128, 4, n).transpose(0, 1, 3, 2))
    if fmt == "e4m3":
        words = by_word.astype(ml_dtypes.float8_e4m3fn).view(np.uint8)
    else:
        c = by_word.astype(ml_dtypes.float4_e2m1fn).view(np.uint8) & 0xF
        words = c[..., 0::2] | (c[..., 1::2] << 4)
    return np.ascontiguousarray(words), np.ascontiguousarray(byte.astype(np.uint8).reshape(k // 512, 16, n))


def unpack_weight(words, scales, fmt):
    g, p, n, _ = words.shape
    if fmt == "e4m3":
        vals = np.ascontiguousarray(words).view(ml_dtypes.float8_e4m3fn).astype(np.float64)
    else:
        nib = np.empty((g, p, n, 4), np.uint8)
        nib[..., 0::2] = words & 0xF
        nib[..., 1::2] = words >> 4
        vals = E2M1[nib]
    vals = vals * np.repeat(np.exp2(scales.astype(np.float64) - 127.0), 8, axis=1)[..., None]
    return vals.transpose(0, 1, 3, 2).reshape(g * 512, n)
def pack4(w):
    words, scales = pack_weight(w, "e2m1")
    return words.reshape(words.shape[0], 128, -1), scales


def unpack4(words, scales):
    return unpack_weight(words.reshape(words.shape[0], 128, -1, 2), scales, "e2m1")


M, J, C = 1024, 2048, 1024


def setup_inputs():
    s, u, t = mx_kscale(J), mx_kscale(M), mx_kscale(C)
    x = np.random.standard_normal((M, C)) * t
    codes = np.random.standard_normal((M, J)) * s
    patch_gain = (0.5 + np.random.random(M)) * u
    book = np.random.standard_normal((J, C)) / (3 * np.sqrt(J)) / s[:, None] * t
    row = np.random.standard_normal((M, M)) / (3 * np.sqrt(M)) / u[:, None]
    chan = np.random.standard_normal((C, 2 * C)) / np.sqrt(C) / t[:, None]
    book_words, book_scales = pack4(book)
    row_words, row_scales = pack4(row)
    chan_words, chan_scales = pack4(chan)
    return {"x": bf(x), "codes": bf(codes), "patch_gain": bf(patch_gain),
            "book_words": book_words, "book_scales": book_scales,
            "row_words": row_words, "row_scales": row_scales,
            "chan_words": chan_words, "chan_scales": chan_scales}


def reference(x, codes, patch_gain, book_words, book_scales, row_words, row_scales, chan_words, chan_scales):
    y = f64(x) + (mxq(f64(codes), 1, "e4m3") @ unpack4(book_words, book_scales))
    e = y * f64(patch_gain)[:, None]
    z = y + (unpack4(row_words, row_scales).T @ mxq(e, 0, "e4m3"))
    h = mxq(z, 1, "e4m3") @ unpack4(chan_words, chan_scales)
    return h[:, :C] * np.tanh(h[:, C:])

@@ -1,0 +1,359 @@
+from contextlib import ExitStack
+
+import concourse.mybir as mybir
+from concourse.masks import make_identity
+
+FLOPS = 2 * 1024 * 1024 * (2048 + 1024 + 2048)
+
+F32 = mybir.dt.float32
+BF16 = mybir.dt.bfloat16
+U32 = mybir.dt.uint32
+I32 = mybir.dt.int32
+U8 = mybir.dt.uint8
+FP8X4 = mybir.dt.float8_e4m3fn_x4
+FP4X4 = mybir.dt.float4_e2m1fn_x4
+ADD = mybir.AluOpType.add
+MULT = mybir.AluOpType.mult
+ACT = mybir.ActivationFunctionType
+
+P = 128
+
+
+def tile_codebook_patch_mixer_t2_kernel(
+    tc, x, codes, patch_gain, book_words, book_scales, row_words, row_scales, chan_words, chan_scales, out
+):
+    nc = tc.nc
+    with ExitStack() as ctx:
+        keep = ctx.enter_context(tc.tile_pool(name="keep", bufs=1))
+        ring = ctx.enter_context(tc.tile_pool(name="ring", bufs=3))
+        psum = ctx.enter_context(tc.psum_pool(name="psum", bufs=8))
+        ctx.enter_context(tc.manual_schedule(engines={mybir.EngineType.PE, mybir.EngineType.SP}))
+
+        def kept(name, shape, dt):
+            return keep.tile(shape, dt, name=name, align_bytes=64)
+
+        craw = [kept("craw%d" % m, [P, 2048], BF16) for m in range(8)]
+        qc = [kept("qc%d" % m, [P, 4, P], U32) for m in range(8)]
+        qcs = [kept("qcs%d" % m, [P, 4, P], U8) for m in range(8)]
+        book = [kept("book%d" % h, [P, 4, 1024], U8) for h in range(2)]
+        bs = kept("bs", [P, 4, 1024], U8)
+        xt = [kept("x%d" % m, [P, 1024], BF16) for m in range(8)]
+        y = {(g, h): kept("y%d%d" % (g, h), [P, 4, 512], F32) for g in range(2) for h in range(2)}
+        eq = {(g, h): kept("eq%d%d" % (g, h), [P, 512], U32) for g in range(2) for h in range(2)}
+        eqs = {(g, h): kept("eqs%d%d" % (g, h), [P, 512], U8) for g in range(2) for h in range(2)}
+        rr = kept("rr", [P, 2, 2048], U8)
+        rs = kept("rs", [P, 2, 1024], U8)
+        rp = [kept("rp%d" % g, [P, 2048], U8) for g in range(2)]
+        rps = [kept("rps%d" % g, [P, 1024], U8) for g in range(2)]
+        wt = [kept("wt%d" % g, [P, 4096], U8) for g in range(2)]
+        ws = kept("ws", [P, 2, 2048], U8)
+        zq = {(k, h): kept("zq%d%d" % (k, h), [P, 2, P], U32) for k in range(4) for h in range(2)}
+        zqs = {(k, h): kept("zqs%d%d" % (k, h), [P, 2, P], U8) for k in range(4) for h in range(2)}
+        ident = kept("ident", [P, P], F32)
+        gain_raw = kept("gain_raw", [P, 2, 4], BF16)
+        gain = kept("gain", [P, 8], F32)
+        warm = kept("warm", [P, 1], F32)
+
+        nc.vector.memset(bs[:].rearrange("p g n -> p (g n)").bitcast(I32), 0)
+        nc.vector.memset(warm[:], 0.0)
+        nc.scalar.activation(out=warm[:], in_=warm[:], func=ACT.Tanh)
+        make_identity(nc, ident[:])
+        nc.vector.memset(rs[:].rearrange("p g n -> p (g n)").bitcast(I32), 0)
+        nc.vector.memset(ws[:].rearrange("p g n -> p (g n)").bitcast(I32), 0)
+
+        codes_v = codes.rearrange("(g p t) j -> g t p j", p=P, t=4)
+        x_v = x.rearrange("(g p t) c -> g t p c", p=P, t=4)
+        out_v = out.rearrange("(g p t) c -> g t p c", p=P, t=4)
+
+        def load_codes(m, parts=1):
+            w = 2048 // parts
+            for i in range(parts):
+                nc.sync.dma_start(out=craw[m][:, i * w : (i + 1) * w], in_=codes_v[m // 4, m % 4][:, i * w : (i + 1) * w])
+
+        def load_x(m):
+            nc.sync.dma_start(out=xt[m][:], in_=x_v[m // 4, m % 4])
+
+        def load_scales(tile, src, passes):
+            dst = tile[:].bitcast(I32)
+            for r in range(4):
+                nc.sync.dma_start(
+                    out=dst[r : P : 32],
+                    in_=src.rearrange("g (q r) n -> r q g n", r=4)[r].bitcast(I32),
+                )
+
+        def load_book(h):
+            nc.sync.dma_start(
+                out=book[h][:].bitcast(I32),
+                in_=book_words[:, :, h * 1024 : (h + 1) * 1024].bitcast(I32).rearrange("g p b -> p g b"),
+            )
+
+        nc.scalar.dma_start(out=gain_raw[:], in_=patch_gain.rearrange("(g p t) -> p g t", p=P, t=4))
+        load_codes(0, 2)
+        load_codes(1)
+        load_scales(bs, book_scales, 4)
+        load_book(0)
+        load_codes(2)
+        load_x(0)
+        nc.sync.dma_start(out=rr[:].bitcast(I32), in_=row_words.bitcast(I32).rearrange("g p b -> p g b"))
+        load_codes(3)
+        load_x(1)
+        load_x(2)
+        load_codes(4)
+        load_book(1)
+        load_scales(rs, row_scales, 2)
+        load_x(3)
+        load_codes(5)
+        load_x(4)
+        load_codes(6)
+        load_x(5)
+        load_codes(7)
+        load_x(6)
+        load_x(7)
+        for g in range(2):
+            nc.sync.dma_start(out=wt[g][:].bitcast(I32), in_=chan_words[g].bitcast(I32))
+        load_scales(ws, chan_scales, 2)
+
+        tps = {}
+        cg = {}
+
+        def t_codes(m):
+            words = craw[m][:].bitcast(F32)
+            for b in range(2):
+                tp = psum.tile([P, 2, 2, P], F32, name="ps")
+                tps[m, b] = tp
+                for i in range(2):
+                    for u in range(2):
+                        w0 = 256 * (2 * b + i)
+                        nc.tensor.transpose(tp[:, i, u, :], words[:, w0 + u : w0 + 256 : 2], ident[:])
+
+        def c_codes(m):
+            cg[m] = ring.tile([P, 4, P, 4], BF16, name="cg", align_bytes=64)
+            dst = cg[m][:].bitcast(F32)
+            for b in range(2):
+                nc.scalar.copy(out=dst[:, 2 * b : 2 * b + 2], in_=tps[m, b][:].rearrange("p i u m -> p i m u"))
+
+        def q_codes(m):
+            nc.vector.quantize_mx(
+                out=qc[m][:].rearrange("p g m -> p (g m)").bitcast(FP8X4),
+                scales=qcs[m][:].rearrange("p g m -> p (g m)"),
+                in_=cg[m][:].rearrange("p g m t -> p (g m t)"),
+            )
+
+        accs = {}
+
+        def m_book(m, h):
+            acc = psum.tile([P, 512], F32, name="ps")
+            accs[m, h] = acc
+            for g in range(4):
+                nc.tensor.matmul_mx(
+                    out=acc[:],
+                    lhsT=qc[m][:, g, :].bitcast(FP8X4),
+                    lhsT_scale=qcs[m][:, g, :],
+                    rhs=book[h][:, g, :].bitcast(FP4X4),
+                    rhs_scale=bs[:, g, h * 512 : (h + 1) * 512],
+                    start=(g == 0),
+                    stop=(g == 3),
+                )
+
+        def y_add(m, h):
+            nc.vector.tensor_tensor(
+                out=y[m // 4, h][:, m % 4, :], in0=accs[m, h][:], in1=xt[m][:, h * 512 : (h + 1) * 512], op=ADD
+            )
+
+        elin = {}
+        eg = {}
+
+        def e_scale(m, h):
+            g, t = m // 4, m % 4
+            if t == 0:
+                elin[g, h] = ring.tile([P, 4, 512], BF16, name="elin", align_bytes=64)
+                eg[g, h] = ring.tile([P, 512, 4], BF16, name="eg", align_bytes=64)
+            nc.scalar.activation(
+                out=elin[g, h][:, t, :], in_=y[g, h][:, t, :], func=ACT.Copy, scale=gain[:, m : m + 1]
+            )
+
+        def e_inter(g, h, j, copy):
+            cols = slice(j * 128, (j + 1) * 128)
+            copy(
+                out=eg[g, h][:, cols, :].rearrange("p (c i) t -> p c t i", i=4),
+                in_=elin[g, h][:, :, cols].rearrange("p t (c i) -> p c t i", i=4),
+            )
+
+        def q_e(g, h):
+            nc.vector.quantize_mx(
+                out=eq[g, h][:].bitcast(FP8X4), scales=eqs[g, h][:], in_=eg[g, h][:].rearrange("p c t -> p (c t)")
+            )
+
+        def r_words(g, half):
+            sl = slice(half * 1024, (half + 1) * 1024)
+            nc.vector.tensor_copy(
+                out=rp[g][:, sl].rearrange("p (t m b) -> p t m b", t=4, b=2),
+                in_=rr[:, g, sl].rearrange("p (m t b) -> p t m b", t=4, b=2),
+            )
+
+        def r_scales(g):
+            nc.vector.tensor_copy(
+                out=rps[g][:].rearrange("p (G t m) -> p G t m", G=2, t=4),
+                in_=rs[:, g, :].rearrange("p (G m t) -> p G t m", G=2, t=4),
+            )
+
+        zacc = {}
+        zt = {}
+
+        def m_row(mo, h):
+            acc = psum.tile([P, 512], F32, name="ps")
+            zacc[mo, h] = acc
+            for g in range(2):
+                nc.tensor.matmul_mx(
+                    out=acc[:],
+                    lhsT=rp[g][:, mo * 256 : (mo + 1) * 256].bitcast(FP4X4),
+                    lhsT_scale=rps[g][:, mo * P : (mo + 1) * P],
+                    rhs=eq[g, h][:].bitcast(FP8X4),
+                    rhs_scale=eqs[g, h][:],
+                    start=(g == 0),
+                    stop=(g == 1),
+                )
+
+        def z_add(mo, h):
+            zt[mo, h] = keep.tile([P, 512], BF16, name="z%d" % mo, align_bytes=64)
+            nc.vector.tensor_tensor(
+                out=zt[mo, h][:].rearrange("p (u q e) -> p u q e", u=2, e=2),
+                in0=zacc[mo, h][:].rearrange("p (q u e) -> p u q e", u=2, e=2),
+                in1=y[mo // 4, h][:, mo % 4, :].rearrange("p (q u e) -> p u q e", u=2, e=2),
+                op=ADD,
+            )
+
+        ztp = {}
+        zg = {}
+
+        def t_z(k, h):
+            tp = psum.tile([P, 2, 2, P], F32, name="ps")
+            ztp[k, h] = tp
+            for i in range(2):
+                words = zt[2 * k + i, h][:].bitcast(F32)
+                for u in range(2):
+                    nc.tensor.transpose(tp[:, i, u, :], words[:, u * P : (u + 1) * P], ident[:])
+
+        def c_z(k, h):
+            zg[k, h] = ring.tile([P, 2, P, 4], BF16, name="zg", align_bytes=64)
+            nc.scalar.copy(out=zg[k, h][:].bitcast(F32), in_=ztp[k, h][:].rearrange("p i u m -> p i m u"))
+
+        def q_z(k, h):
+            nc.vector.quantize_mx(
+                out=zq[k, h][:].rearrange("p i m -> p (i m)").bitcast(FP8X4),
+                scales=zqs[k, h][:].rearrange("p i m -> p (i m)"),
+                in_=zg[k, h][:].rearrange("p i m t -> p (i m t)"),
+            )
+
+        hacc = {}
+
+        def m_chan(mo, n):
+            acc = psum.tile([P, 512], F32, name="ps")
+            hacc[mo, n] = acc
+            for h in range(2):
+                nc.tensor.matmul_mx(
+                    out=acc[:],
+                    lhsT=zq[mo // 2, h][:, mo % 2, :].bitcast(FP8X4),
+                    lhsT_scale=zqs[mo // 2, h][:, mo % 2, :],
+                    rhs=wt[h][:, n * 1024 : (n + 1) * 1024].bitcast(FP4X4),
+                    rhs_scale=ws[:, h, n * 512 : (n + 1) * 512],
+                    start=(h == 0),
+                    stop=(h == 1),
+                )
+
+        def gate(mo, n):
+            th = ring.tile([P, 512], F32, name="th")
+            nc.scalar.activation(out=th[:], in_=hacc[mo, n + 2][:], func=ACT.Tanh)
+            ot = ring.tile([P, 512], F32, name="ot", bufs=6)
+            parts = 2 if (mo, n) == (7, 1) else 1
+            w = 512 // parts
+            for i in range(parts):
+                sl = slice(i * w, (i + 1) * w)
+                nc.vector.tensor_tensor(out=ot[:, sl], in0=hacc[mo, n][:, sl], in1=th[:, sl], op=MULT)
+                nc.sync.dma_start(
+                    out=out_v[mo // 4, mo % 4][:, n * 512 + i * w : n * 512 + (i + 1) * w], in_=ot[:, sl]
+                )
+
+        LAG = 4
+        V, S = nc.vector.tensor_copy, nc.scalar.copy
+        t_codes(0)
+        c_codes(0)
+        nc.vector.tensor_copy(out=gain[:], in_=gain_raw[:].rearrange("p g t -> p (g t)"))
+        q_codes(0)
+        t_codes(1)
+        r_pieces = [lambda g=g, i=i: r_words(g, i) for g in range(2) for i in range(2)]
+        r_pieces += [lambda g=g: r_scales(g) for g in range(2)]
+        inter = {
+            4: [(0, 0, 0, S), (0, 0, 1, V)],
+            5: [(0, 0, 2, S), (0, 0, 3, V)],
+            8: [(0, 1, 0, S), (0, 1, 1, S)],
+            9: [(1, 0, 0, V), (1, 0, 1, V), (1, 0, 2, S), (1, 0, 3, V)],
+            10: [(0, 1, 2, S), (0, 1, 3, S)],
+        }
+        quant = {5: (0, 0), 9: (1, 0), 10: (0, 1)}
+        for m in range(8 + LAG):
+            if m < 8:
+                m_book(m, 0)
+            if m >= LAG:
+                m_book(m - LAG, 1)
+            if m + 1 < 8:
+                c_codes(m + 1)
+            if 1 <= m <= 8:
+                e_scale(m - 1, 0)
+            if m >= LAG + 1:
+                e_scale(m - LAG - 1, 1)
+            if m + 1 < 8:
+                q_codes(m + 1)
+            if m < 8:
+                y_add(m, 0)
+            for piece in inter.get(m, []):
+                e_inter(*piece)
+            if m in quant:
+                q_e(*quant[m])
+            if m >= LAG:
+                y_add(m - LAG, 1)
+            if 1 <= m <= 3:
+                r_pieces.pop(0)()
+                r_pieces.pop(0)()
+            if m + 2 < 8:
+                t_codes(m + 2)
+        def tz(k, h):
+            t_z(k, h)
+            c_z(k, h)
+            q_z(k, h)
+
+        def s3(mo):
+            for n in range(2):
+                m_chan(mo, n + 2)
+                m_chan(mo, n)
+                gate(mo, n)
+
+        for k in range(4):
+            for mo in (2 * k, 2 * k + 1):
+                m_row(mo, 0)
+                z_add(mo, 0)
+                if mo == 0:
+                    e_scale(7, 1)
+                    for j in range(4):
+                        e_inter(1, 1, j, S)
+                if mo == 6:
+                    q_e(1, 1)
+            if k == 2:
+                tz(0, 0)
+                tz(1, 0)
+        for k in range(4):
+            for mo in (2 * k, 2 * k + 1):
+                m_row(mo, 1)
+                z_add(mo, 1)
+            if k == 0:
+                tz(2, 0)
+                tz(3, 0)
+            if k == 2:
+                tz(0, 1)
+                tz(1, 1)
+            if k == 3:
+                s3(0)
+        tz(2, 1)
+        tz(3, 1)
+        for mo in range(1, 8):
+            s3(mo)

@@ -17,6 +17,18 @@ MULT = mybir.AluOpType.mult
 ACT = mybir.ActivationFunctionType
 
 P = 128
+ORDER = """
+W0 T0 C00 T1 C01 C10 Q0 R0 C11 A00 Q1 W2 R2 R1 T2 Y00 g C20 A10 R3 C21 A01 W3 Q2 Y10 A11 E00 X4 E10
+A21 Y01 Y11 E01 T3 E11 Y21 T4 C30 R4 C31 A20 R5 C40 Q3 C41 T5 X6 W7 Q4 A30 Y20 C50 A40 C51 Y30 E20
+Q5 T6 E30 Y40 T7 C60 J000 C61 J001 A31 J002 C70 Q6 C71 A50 Y31 E40 Q7 A60 I003 Y50 E21 A70 K00 E50
+Y60 E31 A41 Y70 E60 J010 A51 E70 Y41 I012 J100 A61 J102 I101 Y51 I103 A71 Y61 E41 K10 B00 E51 Y71
+E61 B10 J011 E71 z00 B20 I013 J111 B30 J113 I110 B40 z10 B50 I112 K01 U00 K11 B01 D00 z20 B11 z30
+z40 U10 B60 z50 D10 B21 z01 B31 z11 U01 q00 z60 B41 D01 z21 B51 q01 B61 z31 H02 z41 H00 G00 z51 H03
+z61 H01 G01 F00 U20 U11 q10 U21 D20 F01 H12 D11 q20 H10 D21 q11 H13 G10 q21 H11 G11 F10 H22 H20 F11
+G20 H23 H21 F20 G21 B70 B71 F21 H32 z70 H30 z71 G30 H33 H31 F30 G31 U30 U31 F31 D30 H42 D31 H40 q30
+H43 G40 q31 H41 F40 G41 H52 H50 F41 G50 H53 H51 F50 G51 H62 H60 F51 G60 H63 H61 F60 G61 H72 H70 F61
+G70 H73 H71 F70 G71 F71
+"""
 
 
 def tile_codebook_patch_mixer_t2_kernel(
@@ -27,7 +39,7 @@ def tile_codebook_patch_mixer_t2_kernel(
         keep = ctx.enter_context(tc.tile_pool(name="keep", bufs=1))
         ring = ctx.enter_context(tc.tile_pool(name="ring", bufs=3))
         psum = ctx.enter_context(tc.psum_pool(name="psum", bufs=8))
-        ctx.enter_context(tc.manual_schedule(engines={mybir.EngineType.PE, mybir.EngineType.SP}))
+        ctx.enter_context(tc.manual_schedule())
 
         def kept(name, shape, dt):
             return keep.tile(shape, dt, name=name, align_bytes=64)
@@ -54,8 +66,8 @@ def tile_codebook_patch_mixer_t2_kernel(
         gain = kept("gain", [P, 8], F32)
         warm = kept("warm", [P, 1], F32)
 
-        nc.vector.memset(bs[:].rearrange("p g n -> p (g n)").bitcast(I32), 0)
         nc.vector.memset(warm[:], 0.0)
+        nc.vector.memset(bs[:].rearrange("p g n -> p (g n)").bitcast(I32), 0)
         nc.scalar.activation(out=warm[:], in_=warm[:], func=ACT.Tanh)
         make_identity(nc, ident[:])
         nc.vector.memset(rs[:].rearrange("p g n -> p (g n)").bitcast(I32), 0)
@@ -73,7 +85,7 @@ def tile_codebook_patch_mixer_t2_kernel(
         def load_x(m):
             nc.sync.dma_start(out=xt[m][:], in_=x_v[m // 4, m % 4])
 
-        def load_scales(tile, src, passes):
+        def load_scales(tile, src):
             dst = tile[:].bitcast(I32)
             for r in range(4):
                 nc.sync.dma_start(
@@ -90,31 +102,37 @@ def tile_codebook_patch_mixer_t2_kernel(
         nc.scalar.dma_start(out=gain_raw[:], in_=patch_gain.rearrange("(g p t) -> p g t", p=P, t=4))
         load_codes(0, 2)
         load_codes(1)
-        load_scales(bs, book_scales, 4)
+        load_scales(bs, book_scales)
         load_book(0)
-        load_codes(2)
-        load_x(0)
         nc.sync.dma_start(out=rr[:].bitcast(I32), in_=row_words.bitcast(I32).rearrange("g p b -> p g b"))
+        load_codes(2)
+        load_book(1)
+        load_x(0)
         load_codes(3)
         load_x(1)
-        load_x(2)
         load_codes(4)
-        load_book(1)
-        load_scales(rs, row_scales, 2)
-        load_x(3)
+        load_x(2)
         load_codes(5)
-        load_x(4)
+        load_scales(rs, row_scales)
+        load_x(3)
         load_codes(6)
-        load_x(5)
         load_codes(7)
+        load_x(4)
+        load_x(5)
         load_x(6)
         load_x(7)
-        for g in range(2):
-            nc.sync.dma_start(out=wt[g][:].bitcast(I32), in_=chan_words[g].bitcast(I32))
-        load_scales(ws, chan_scales, 2)
+        nc.sync.dma_start(out=wt[0][:].bitcast(I32), in_=chan_words[0].bitcast(I32))
+        nc.sync.dma_start(out=wt[1][:].bitcast(I32), in_=chan_words[1].bitcast(I32))
+        load_scales(ws, chan_scales)
 
         tps = {}
         cg = {}
+
+        cw = {}
+
+        def w_codes(m, copy):
+            cw[m] = ring.tile([P, 4, 2, P], F32, name="cw", bufs=2)
+            copy(out=cw[m][:], in_=craw[m][:].bitcast(F32).rearrange("p (g q u) -> p g u q", g=4, u=2))
 
         def t_codes(m):
             words = craw[m][:].bitcast(F32)
@@ -124,13 +142,17 @@ def tile_codebook_patch_mixer_t2_kernel(
                 for i in range(2):
                     for u in range(2):
                         w0 = 256 * (2 * b + i)
-                        nc.tensor.transpose(tp[:, i, u, :], words[:, w0 + u : w0 + 256 : 2], ident[:])
+                        src = cw[m][:, 2 * b + i, u, :] if m in cw else words[:, w0 + u : w0 + 256 : 2]
+                        nc.tensor.transpose(tp[:, i, u, :], src, ident[:])
 
-        def c_codes(m):
-            cg[m] = ring.tile([P, 4, P, 4], BF16, name="cg", align_bytes=64)
-            dst = cg[m][:].bitcast(F32)
-            for b in range(2):
-                nc.scalar.copy(out=dst[:, 2 * b : 2 * b + 2], in_=tps[m, b][:].rearrange("p i u m -> p i m u"))
+        def c_codes(m, b):
+            if b == 0:
+                cg[m] = ring.tile([P, 4, P, 4], BF16, name="cg", align_bytes=64)
+            copy = nc.vector.tensor_copy if (m, b) == (0, 1) else nc.scalar.copy
+            copy(
+                out=cg[m][:].bitcast(F32)[:, 2 * b : 2 * b + 2],
+                in_=tps[m, b][:].rearrange("p i u m -> p i m u"),
+            )
 
         def q_codes(m):
             nc.vector.quantize_mx(
@@ -215,7 +237,9 @@ def tile_codebook_patch_mixer_t2_kernel(
                 )
 
         def z_add(mo, h):
-            zt[mo, h] = keep.tile([P, 512], BF16, name="z%d" % mo, align_bytes=64)
+            zt[mo, h] = keep.tile(
+                [P, 512], BF16, name="z%d%d" % (mo, h), tag="z%d" % mo if h else "craw%d" % mo, align_bytes=64
+            )
             nc.vector.tensor_tensor(
                 out=zt[mo, h][:].rearrange("p (u q e) -> p u q e", u=2, e=2),
                 in0=zacc[mo, h][:].rearrange("p (q u e) -> p u q e", u=2, e=2),
@@ -261,99 +285,46 @@ def tile_codebook_patch_mixer_t2_kernel(
                     stop=(h == 1),
                 )
 
+        th = {}
+
         def gate(mo, n):
-            th = ring.tile([P, 512], F32, name="th")
-            nc.scalar.activation(out=th[:], in_=hacc[mo, n + 2][:], func=ACT.Tanh)
+            th[mo, n] = ring.tile([P, 512], F32, name="th", bufs=4)
+            nc.scalar.activation(out=th[mo, n][:], in_=hacc[mo, n + 2][:], func=ACT.Tanh)
+
+        def finish(mo, n):
             ot = ring.tile([P, 512], F32, name="ot", bufs=6)
             parts = 2 if (mo, n) == (7, 1) else 1
             w = 512 // parts
             for i in range(parts):
                 sl = slice(i * w, (i + 1) * w)
-                nc.vector.tensor_tensor(out=ot[:, sl], in0=hacc[mo, n][:, sl], in1=th[:, sl], op=MULT)
+                nc.vector.tensor_tensor(out=ot[:, sl], in0=hacc[mo, n][:, sl], in1=th[mo, n][:, sl], op=MULT)
                 nc.sync.dma_start(
                     out=out_v[mo // 4, mo % 4][:, n * 512 + i * w : n * 512 + (i + 1) * w], in_=ot[:, sl]
                 )
 
-        LAG = 4
         V, S = nc.vector.tensor_copy, nc.scalar.copy
-        t_codes(0)
-        c_codes(0)
-        nc.vector.tensor_copy(out=gain[:], in_=gain_raw[:].rearrange("p g t -> p (g t)"))
-        q_codes(0)
-        t_codes(1)
-        r_pieces = [lambda g=g, i=i: r_words(g, i) for g in range(2) for i in range(2)]
-        r_pieces += [lambda g=g: r_scales(g) for g in range(2)]
-        inter = {
-            4: [(0, 0, 0, S), (0, 0, 1, V)],
-            5: [(0, 0, 2, S), (0, 0, 3, V)],
-            8: [(0, 1, 0, S), (0, 1, 1, S)],
-            9: [(1, 0, 0, V), (1, 0, 1, V), (1, 0, 2, S), (1, 0, 3, V)],
-            10: [(0, 1, 2, S), (0, 1, 3, S)],
+        run = {
+            "g": lambda: nc.vector.tensor_copy(out=gain[:], in_=gain_raw[:].rearrange("p g t -> p (g t)")),
+            "T": t_codes,
+            "W": lambda m: w_codes(m, S),
+            "X": lambda m: w_codes(m, V),
+            "C": c_codes,
+            "Q": q_codes,
+            "A": m_book,
+            "Y": y_add,
+            "E": e_scale,
+            "I": lambda g, h, j: e_inter(g, h, j, S),
+            "J": lambda g, h, j: e_inter(g, h, j, V),
+            "K": q_e,
+            "R": lambda i: r_words(i // 2, i % 2) if i < 4 else r_scales(i - 4),
+            "B": m_row,
+            "z": z_add,
+            "U": t_z,
+            "D": c_z,
+            "q": q_z,
+            "H": m_chan,
+            "G": gate,
+            "F": finish,
         }
-        quant = {5: (0, 0), 9: (1, 0), 10: (0, 1)}
-        for m in range(8 + LAG):
-            if m < 8:
-                m_book(m, 0)
-            if m >= LAG:
-                m_book(m - LAG, 1)
-            if m + 1 < 8:
-                c_codes(m + 1)
-            if 1 <= m <= 8:
-                e_scale(m - 1, 0)
-            if m >= LAG + 1:
-                e_scale(m - LAG - 1, 1)
-            if m + 1 < 8:
-                q_codes(m + 1)
-            if m < 8:
-                y_add(m, 0)
-            for piece in inter.get(m, []):
-                e_inter(*piece)
-            if m in quant:
-                q_e(*quant[m])
-            if m >= LAG:
-                y_add(m - LAG, 1)
-            if 1 <= m <= 3:
-                r_pieces.pop(0)()
-                r_pieces.pop(0)()
-            if m + 2 < 8:
-                t_codes(m + 2)
-        def tz(k, h):
-            t_z(k, h)
-            c_z(k, h)
-            q_z(k, h)
-
-        def s3(mo):
-            for n in range(2):
-                m_chan(mo, n + 2)
-                m_chan(mo, n)
-                gate(mo, n)
-
-        for k in range(4):
-            for mo in (2 * k, 2 * k + 1):
-                m_row(mo, 0)
-                z_add(mo, 0)
-                if mo == 0:
-                    e_scale(7, 1)
-                    for j in range(4):
-                        e_inter(1, 1, j, S)
-                if mo == 6:
-                    q_e(1, 1)
-            if k == 2:
-                tz(0, 0)
-                tz(1, 0)
-        for k in range(4):
-            for mo in (2 * k, 2 * k + 1):
-                m_row(mo, 1)
-                z_add(mo, 1)
-            if k == 0:
-                tz(2, 0)
-                tz(3, 0)
-            if k == 2:
-                tz(0, 1)
-                tz(1, 1)
-            if k == 3:
-                s3(0)
-        tz(2, 1)
-        tz(3, 1)
-        for mo in range(1, 8):
-            s3(mo)
+        for token in ORDER.split():
+            run[token[0]](*[int(n) for n in token[1:]])

from contextlib import ExitStack

import concourse.mybir as mybir
from concourse.masks import make_identity

FLOPS = 2 * 1024 * 1024 * (2048 + 1024 + 2048)

F32 = mybir.dt.float32
BF16 = mybir.dt.bfloat16
U32 = mybir.dt.uint32
I32 = mybir.dt.int32
U8 = mybir.dt.uint8
FP8X4 = mybir.dt.float8_e4m3fn_x4
FP4X4 = mybir.dt.float4_e2m1fn_x4
ADD = mybir.AluOpType.add
MULT = mybir.AluOpType.mult
ACT = mybir.ActivationFunctionType

P = 128
ORDER = """
W0 T0 C00 T1 C01 C10 Q0 R0 C11 A00 Q1 W2 R2 R1 T2 Y00 g C20 A10 R3 C21 A01 W3 Q2 Y10 A11 E00 X4 E10
A21 Y01 Y11 E01 T3 E11 Y21 T4 C30 R4 C31 A20 R5 C40 Q3 C41 T5 X6 W7 Q4 A30 Y20 C50 A40 C51 Y30 E20
Q5 T6 E30 Y40 T7 C60 J000 C61 J001 A31 J002 C70 Q6 C71 A50 Y31 E40 Q7 A60 I003 Y50 E21 A70 K00 E50
Y60 E31 A41 Y70 E60 J010 A51 E70 Y41 I012 J100 A61 J102 I101 Y51 I103 A71 Y61 E41 K10 B00 E51 Y71
E61 B10 J011 E71 z00 B20 I013 J111 B30 J113 I110 B40 z10 B50 I112 K01 U00 K11 B01 D00 z20 B11 z30
z40 U10 B60 z50 D10 B21 z01 B31 z11 U01 q00 z60 B41 D01 z21 B51 q01 B61 z31 H02 z41 H00 G00 z51 H03
z61 H01 G01 F00 U20 U11 q10 U21 D20 F01 H12 D11 q20 H10 D21 q11 H13 G10 q21 H11 G11 F10 H22 H20 F11
G20 H23 H21 F20 G21 B70 B71 F21 H32 z70 H30 z71 G30 H33 H31 F30 G31 U30 U31 F31 D30 H42 D31 H40 q30
H43 G40 q31 H41 F40 G41 H52 H50 F41 G50 H53 H51 F50 G51 H62 H60 F51 G60 H63 H61 F60 G61 H72 H70 F61
G70 H73 H71 F70 G71 F71
"""


def tile_codebook_patch_mixer_t2_kernel(
    tc, x, codes, patch_gain, book_words, book_scales, row_words, row_scales, chan_words, chan_scales, out
):
    nc = tc.nc
    with ExitStack() as ctx:
        keep = ctx.enter_context(tc.tile_pool(name="keep", bufs=1))
        ring = ctx.enter_context(tc.tile_pool(name="ring", bufs=3))
        psum = ctx.enter_context(tc.psum_pool(name="psum", bufs=8))
        ctx.enter_context(tc.manual_schedule())

        def kept(name, shape, dt):
            return keep.tile(shape, dt, name=name, align_bytes=64)

        craw = [kept("craw%d" % m, [P, 2048], BF16) for m in range(8)]
        qc = [kept("qc%d" % m, [P, 4, P], U32) for m in range(8)]
        qcs = [kept("qcs%d" % m, [P, 4, P], U8) for m in range(8)]
        book = [kept("book%d" % h, [P, 4, 1024], U8) for h in range(2)]
        bs = kept("bs", [P, 4, 1024], U8)
        xt = [kept("x%d" % m, [P, 1024], BF16) for m in range(8)]
        y = {(g, h): kept("y%d%d" % (g, h), [P, 4, 512], F32) for g in range(2) for h in range(2)}
        eq = {(g, h): kept("eq%d%d" % (g, h), [P, 512], U32) for g in range(2) for h in range(2)}
        eqs = {(g, h): kept("eqs%d%d" % (g, h), [P, 512], U8) for g in range(2) for h in range(2)}
        rr = kept("rr", [P, 2, 2048], U8)
        rs = kept("rs", [P, 2, 1024], U8)
        rp = [kept("rp%d" % g, [P, 2048], U8) for g in range(2)]
        rps = [kept("rps%d" % g, [P, 1024], U8) for g in range(2)]
        wt = [kept("wt%d" % g, [P, 4096], U8) for g in range(2)]
        ws = kept("ws", [P, 2, 2048], U8)
        zq = {(k, h): kept("zq%d%d" % (k, h), [P, 2, P], U32) for k in range(4) for h in range(2)}
        zqs = {(k, h): kept("zqs%d%d" % (k, h), [P, 2, P], U8) for k in range(4) for h in range(2)}
        ident = kept("ident", [P, P], F32)
        gain_raw = kept("gain_raw", [P, 2, 4], BF16)
        gain = kept("gain", [P, 8], F32)
        warm = kept("warm", [P, 1], F32)

        nc.vector.memset(warm[:], 0.0)
        nc.vector.memset(bs[:].rearrange("p g n -> p (g n)").bitcast(I32), 0)
        nc.scalar.activation(out=warm[:], in_=warm[:], func=ACT.Tanh)
        make_identity(nc, ident[:])
        nc.vector.memset(rs[:].rearrange("p g n -> p (g n)").bitcast(I32), 0)
        nc.vector.memset(ws[:].rearrange("p g n -> p (g n)").bitcast(I32), 0)

        codes_v = codes.rearrange("(g p t) j -> g t p j", p=P, t=4)
        x_v = x.rearrange("(g p t) c -> g t p c", p=P, t=4)
        out_v = out.rearrange("(g p t) c -> g t p c", p=P, t=4)

        def load_codes(m, parts=1):
            w = 2048 // parts
            for i in range(parts):
                nc.sync.dma_start(out=craw[m][:, i * w : (i + 1) * w], in_=codes_v[m // 4, m % 4][:, i * w : (i + 1) * w])

        def load_x(m):
            nc.sync.dma_start(out=xt[m][:], in_=x_v[m // 4, m % 4])

        def load_scales(tile, src):
            dst = tile[:].bitcast(I32)
            for r in range(4):
                nc.sync.dma_start(
                    out=dst[r : P : 32],
                    in_=src.rearrange("g (q r) n -> r q g n", r=4)[r].bitcast(I32),
                )

        def load_book(h):
            nc.sync.dma_start(
                out=book[h][:].bitcast(I32),
                in_=book_words[:, :, h * 1024 : (h + 1) * 1024].bitcast(I32).rearrange("g p b -> p g b"),
            )

        nc.scalar.dma_start(out=gain_raw[:], in_=patch_gain.rearrange("(g p t) -> p g t", p=P, t=4))
        load_codes(0, 2)
        load_codes(1)
        load_scales(bs, book_scales)
        load_book(0)
        nc.sync.dma_start(out=rr[:].bitcast(I32), in_=row_words.bitcast(I32).rearrange("g p b -> p g b"))
        load_codes(2)
        load_book(1)
        load_x(0)
        load_codes(3)
        load_x(1)
        load_codes(4)
        load_x(2)
        load_codes(5)
        load_scales(rs, row_scales)
        load_x(3)
        load_codes(6)
        load_codes(7)
        load_x(4)
        load_x(5)
        load_x(6)
        load_x(7)
        nc.sync.dma_start(out=wt[0][:].bitcast(I32), in_=chan_words[0].bitcast(I32))
        nc.sync.dma_start(out=wt[1][:].bitcast(I32), in_=chan_words[1].bitcast(I32))
        load_scales(ws, chan_scales)

        tps = {}
        cg = {}

        cw = {}

        def w_codes(m, copy):
            cw[m] = ring.tile([P, 4, 2, P], F32, name="cw", bufs=2)
            copy(out=cw[m][:], in_=craw[m][:].bitcast(F32).rearrange("p (g q u) -> p g u q", g=4, u=2))

        def t_codes(m):
            words = craw[m][:].bitcast(F32)
            for b in range(2):
                tp = psum.tile([P, 2, 2, P], F32, name="ps")
                tps[m, b] = tp
                for i in range(2):
                    for u in range(2):
                        w0 = 256 * (2 * b + i)
                        src = cw[m][:, 2 * b + i, u, :] if m in cw else words[:, w0 + u : w0 + 256 : 2]
                        nc.tensor.transpose(tp[:, i, u, :], src, ident[:])

        def c_codes(m, b):
            if b == 0:
                cg[m] = ring.tile([P, 4, P, 4], BF16, name="cg", align_bytes=64)
            copy = nc.vector.tensor_copy if (m, b) == (0, 1) else nc.scalar.copy
            copy(
                out=cg[m][:].bitcast(F32)[:, 2 * b : 2 * b + 2],
                in_=tps[m, b][:].rearrange("p i u m -> p i m u"),
            )

        def q_codes(m):
            nc.vector.quantize_mx(
                out=qc[m][:].rearrange("p g m -> p (g m)").bitcast(FP8X4),
                scales=qcs[m][:].rearrange("p g m -> p (g m)"),
                in_=cg[m][:].rearrange("p g m t -> p (g m t)"),
            )

        accs = {}

        def m_book(m, h):
            acc = psum.tile([P, 512], F32, name="ps")
            accs[m, h] = acc
            for g in range(4):
                nc.tensor.matmul_mx(
                    out=acc[:],
                    lhsT=qc[m][:, g, :].bitcast(FP8X4),
                    lhsT_scale=qcs[m][:, g, :],
                    rhs=book[h][:, g, :].bitcast(FP4X4),
                    rhs_scale=bs[:, g, h * 512 : (h + 1) * 512],
                    start=(g == 0),
                    stop=(g == 3),
                )

        def y_add(m, h):
            nc.vector.tensor_tensor(
                out=y[m // 4, h][:, m % 4, :], in0=accs[m, h][:], in1=xt[m][:, h * 512 : (h + 1) * 512], op=ADD
            )

        elin = {}
        eg = {}

        def e_scale(m, h):
            g, t = m // 4, m % 4
            if t == 0:
                elin[g, h] = ring.tile([P, 4, 512], BF16, name="elin", align_bytes=64)
                eg[g, h] = ring.tile([P, 512, 4], BF16, name="eg", align_bytes=64)
            nc.scalar.activation(
                out=elin[g, h][:, t, :], in_=y[g, h][:, t, :], func=ACT.Copy, scale=gain[:, m : m + 1]
            )

        def e_inter(g, h, j, copy):
            cols = slice(j * 128, (j + 1) * 128)
            copy(
                out=eg[g, h][:, cols, :].rearrange("p (c i) t -> p c t i", i=4),
                in_=elin[g, h][:, :, cols].rearrange("p t (c i) -> p c t i", i=4),
            )

        def q_e(g, h):
            nc.vector.quantize_mx(
                out=eq[g, h][:].bitcast(FP8X4), scales=eqs[g, h][:], in_=eg[g, h][:].rearrange("p c t -> p (c t)")
            )

        def r_words(g, half):
            sl = slice(half * 1024, (half + 1) * 1024)
            nc.vector.tensor_copy(
                out=rp[g][:, sl].rearrange("p (t m b) -> p t m b", t=4, b=2),
                in_=rr[:, g, sl].rearrange("p (m t b) -> p t m b", t=4, b=2),
            )

        def r_scales(g):
            nc.vector.tensor_copy(
                out=rps[g][:].rearrange("p (G t m) -> p G t m", G=2, t=4),
                in_=rs[:, g, :].rearrange("p (G m t) -> p G t m", G=2, t=4),
            )

        zacc = {}
        zt = {}

        def m_row(mo, h):
            acc = psum.tile([P, 512], F32, name="ps")
            zacc[mo, h] = acc
            for g in range(2):
                nc.tensor.matmul_mx(
                    out=acc[:],
                    lhsT=rp[g][:, mo * 256 : (mo + 1) * 256].bitcast(FP4X4),
                    lhsT_scale=rps[g][:, mo * P : (mo + 1) * P],
                    rhs=eq[g, h][:].bitcast(FP8X4),
                    rhs_scale=eqs[g, h][:],
                    start=(g == 0),
                    stop=(g == 1),
                )

        def z_add(mo, h):
            zt[mo, h] = keep.tile(
                [P, 512], BF16, name="z%d%d" % (mo, h), tag="z%d" % mo if h else "craw%d" % mo, align_bytes=64
            )
            nc.vector.tensor_tensor(
                out=zt[mo, h][:].rearrange("p (u q e) -> p u q e", u=2, e=2),
                in0=zacc[mo, h][:].rearrange("p (q u e) -> p u q e", u=2, e=2),
                in1=y[mo // 4, h][:, mo % 4, :].rearrange("p (q u e) -> p u q e", u=2, e=2),
                op=ADD,
            )

        ztp = {}
        zg = {}

        def t_z(k, h):
            tp = psum.tile([P, 2, 2, P], F32, name="ps")
            ztp[k, h] = tp
            for i in range(2):
                words = zt[2 * k + i, h][:].bitcast(F32)
                for u in range(2):
                    nc.tensor.transpose(tp[:, i, u, :], words[:, u * P : (u + 1) * P], ident[:])

        def c_z(k, h):
            zg[k, h] = ring.tile([P, 2, P, 4], BF16, name="zg", align_bytes=64)
            nc.scalar.copy(out=zg[k, h][:].bitcast(F32), in_=ztp[k, h][:].rearrange("p i u m -> p i m u"))

        def q_z(k, h):
            nc.vector.quantize_mx(
                out=zq[k, h][:].rearrange("p i m -> p (i m)").bitcast(FP8X4),
                scales=zqs[k, h][:].rearrange("p i m -> p (i m)"),
                in_=zg[k, h][:].rearrange("p i m t -> p (i m t)"),
            )

        hacc = {}

        def m_chan(mo, n):
            acc = psum.tile([P, 512], F32, name="ps")
            hacc[mo, n] = acc
            for h in range(2):
                nc.tensor.matmul_mx(
                    out=acc[:],
                    lhsT=zq[mo // 2, h][:, mo % 2, :].bitcast(FP8X4),
                    lhsT_scale=zqs[mo // 2, h][:, mo % 2, :],
                    rhs=wt[h][:, n * 1024 : (n + 1) * 1024].bitcast(FP4X4),
                    rhs_scale=ws[:, h, n * 512 : (n + 1) * 512],
                    start=(h == 0),
                    stop=(h == 1),
                )

        th = {}

        def gate(mo, n):
            th[mo, n] = ring.tile([P, 512], F32, name="th", bufs=4)
            nc.scalar.activation(out=th[mo, n][:], in_=hacc[mo, n + 2][:], func=ACT.Tanh)

        def finish(mo, n):
            ot = ring.tile([P, 512], F32, name="ot", bufs=6)
            parts = 2 if (mo, n) == (7, 1) else 1
            w = 512 // parts
            for i in range(parts):
                sl = slice(i * w, (i + 1) * w)
                nc.vector.tensor_tensor(out=ot[:, sl], in0=hacc[mo, n][:, sl], in1=th[mo, n][:, sl], op=MULT)
                nc.sync.dma_start(
                    out=out_v[mo // 4, mo % 4][:, n * 512 + i * w : n * 512 + (i + 1) * w], in_=ot[:, sl]
                )

        V, S = nc.vector.tensor_copy, nc.scalar.copy
        run = {
            "g": lambda: nc.vector.tensor_copy(out=gain[:], in_=gain_raw[:].rearrange("p g t -> p (g t)")),
            "T": t_codes,
            "W": lambda m: w_codes(m, S),
            "X": lambda m: w_codes(m, V),
            "C": c_codes,
            "Q": q_codes,
            "A": m_book,
            "Y": y_add,
            "E": e_scale,
            "I": lambda g, h, j: e_inter(g, h, j, S),
            "J": lambda g, h, j: e_inter(g, h, j, V),
            "K": q_e,
            "R": lambda i: r_words(i // 2, i % 2) if i < 4 else r_scales(i - 4),
            "B": m_row,
            "z": z_add,
            "U": t_z,
            "D": c_z,
            "q": q_z,
            "H": m_chan,
            "G": gate,
            "F": finish,
        }
        for token in ORDER.split():
            run[token[0]](*[int(n) for n in token[1:]])
